import numpy as np
import ml_dtypes


def mxq(x, axis, fmt="e4m3"):
    dtype, down = {"e4m3": (ml_dtypes.float8_e4m3fn, 7), "e5m2": (ml_dtypes.float8_e5m2, 14)}[fmt]
    v = np.moveaxis(np.asarray(x, np.float32).astype(ml_dtypes.bfloat16).astype(np.float64), axis, -1)
    blocks = v.reshape(v.shape[:-1] + (-1, 32))
    amax = np.abs(blocks).max(-1, keepdims=True)
    byte = np.maximum(np.where(amax > 0, np.frexp(amax)[1] - 1 + 127, 0) - down, 1)
    scale = np.exp2(byte - 127.0)
    codes = (blocks / scale).astype(np.float32).astype(dtype).astype(np.float64)
    return np.moveaxis((codes * scale).reshape(v.shape), -1, axis)


WIDE = False


def mx_kscale(k):
    if not WIDE:
        return np.ones(k)
    levels = np.array([10, -10, 5, -5, 0])
    if k % 512:
        return np.exp2(np.random.permutation(np.resize(levels, k // 32))).repeat(32)
    a = np.empty((k // 512, 16))
    for p in range(k // 512):
        a[p, :8] = np.random.permutation(np.resize(levels, 8))
        for g in range(8):
            far = levels[np.abs(levels - a[p, g]) >= 10]
            a[p, g + 8] = far[np.random.randint(len(far))]
    return np.exp2(a.ravel()).repeat(32)


def f64(x):
    return np.asarray(x).astype(np.float64)


def striped8(idx):
    return np.concatenate([x.reshape(-1, 16).T for x in idx]).astype(np.uint16)


def runs(offs, k):
    lists = np.stack([offs[16 * r : 16 * r + 16].T.reshape(-1) for r in range(8)]).astype(np.int64)
    return lists[np.arange(k) % 512 // 64]


def pack_weight(w):
    k, n = w.shape
    w = f64(np.asarray(w, np.float32).astype(ml_dtypes.bfloat16)).reshape(k // 32, 32, n)
    amax = np.abs(w).max(1)
    byte = np.clip(np.where(amax > 0, np.frexp(amax)[1] - 1 + 127 - 7, 1), 1, 254)
    scaled = (w * np.exp2(127.0 - byte)[:, None, :]).reshape(k, n).astype(np.float32)
    words = np.ascontiguousarray(scaled.reshape(k // 512, 128, 4, n).transpose(0, 1, 3, 2)).astype(ml_dtypes.float8_e4m3fn).view(np.uint8)
    return words, np.ascontiguousarray(byte.astype(np.uint8).reshape(k // 512, 16, n))


def unpack_weight(words, scales):
    g, p, n, _ = words.shape
    vals = np.ascontiguousarray(words).view(ml_dtypes.float8_e4m3fn).astype(np.float64) * np.repeat(np.exp2(scales.astype(np.float64) - 127.0), 8, axis=1)[..., None]
    return vals.transpose(0, 1, 3, 2).reshape(g * 512, n)


K, T, S, N, H, W = 512, 2048, 512, 512, 512, 256


def setup_inputs():
    n = np.random.standard_normal
    s = mx_kscale(K)[:, None]
    u = mx_kscale(H)
    packed_xT = pack_weight(n((K, T)) * s)
    perm = np.stack([np.random.permutation(S) for _ in range(8)])
    return {
        "x_words": packed_xT[0],
        "x_scales": packed_xT[1],
        "w1": (n((K, H)) / np.sqrt(K) / s).astype(np.float32),
        "gn": (np.random.uniform(0.5, 1.5, (H, 1)) * u[:, None]).astype(np.float32),
        "w2": (n((H, N)) / np.sqrt(H) / u[:, None]).astype(np.float32),
        "offs": striped8(np.random.randint(0, T, (8, S))),
        "n1": striped8(perm[:, :W]),
        "n2": striped8(perm[:, W:]),
        "n3": striped8(np.stack([np.random.permutation(S) for _ in range(8)])),
        "n4": striped8(np.stack([np.random.permutation(S) for _ in range(8)])),
    }


def reference(x_words, x_scales, w1, gn, w2, offs, n1, n2, n3, n4):
    xq = unpack_weight(x_words, x_scales)[np.arange(K)[:, None], runs(offs, K)]
    y = mxq(f64(w1), 0, "e4m3").T @ xq
    pa = y[np.arange(H)[:, None], runs(n1, H)]
    pb = y[np.arange(H)[:, None], runs(n2, H)]
    rb = pa * pb
    ra = pa + pb
    ds = np.zeros((H, S))
    ds[np.arange(H)[:, None], runs(n1, H)] = ra
    dt = ds.copy()
    dt[np.arange(H)[:, None], runs(n2, H)] = rb
    z = f64(gn) * dt
    h = mxq(f64(w2), 0, "e4m3").T @ mxq(z, 0, "e4m3")
    return 0.75 * ((h - (h[np.arange(N)[:, None], runs(n3, N)])) * (h - (h[np.arange(N)[:, None], runs(n4, N)])))

@@ -1,0 +1,173 @@
+from contextlib import ExitStack
+
+import concourse.mybir as mybir
+
+K, T, S, N, H, W = 512, 2048, 512, 512, 512, 256
+FLOPS = 2 * K * H * S + 2 * H * N * S
+
+F32 = mybir.dt.float32
+BF16 = mybir.dt.bfloat16
+I32 = mybir.dt.int32
+U32 = mybir.dt.uint32
+U16 = mybir.dt.uint16
+U8 = mybir.dt.uint8
+FP8X4 = mybir.dt.float8_e4m3fn_x4
+ALU = mybir.AluOpType
+COPY = mybir.ActivationFunctionType.Copy
+
+P = 128
+PACK = 4
+HALF = S // 2
+GROUP = 16
+
+
+def tile_picked_hashbondquad_none_p_kernel(tc, x_words, x_scales, w1, gn, w2, offs, n1, n2, n3, n4, out):
+    nc = tc.nc
+    halves = [slice(0, HALF), slice(HALF, S)]
+    list_halves = [slice(0, HALF // GROUP), slice(HALF // GROUP, S // GROUP)]
+
+    with ExitStack() as ctx:
+        keep = ctx.enter_context(tc.tile_pool(name="keep", bufs=1))
+        psum = ctx.enter_context(tc.psum_pool(name="psum", bufs=1))
+
+        def load_list(src, name):
+            tile = keep.tile(list(src.shape), U16, name=name)
+            nc.sync.dma_start(tile[:], src)
+            return tile
+
+        def deal(engine_copy, grouped, raw):
+            engine_copy(
+                out=grouped[:].rearrange("p (t m j) -> p m t j", t=PACK, j=PACK),
+                in_=raw[:].rearrange("p j (m t) -> p m t j", t=PACK),
+            )
+
+        offs_sb = load_list(offs, "offs_sb")
+        scale_table = keep.tile([P, T], U8, name="scale_table")
+        nc.vector.memset(scale_table[:].bitcast(I32), 0)
+
+        w1_raw = keep.tile([P, PACK, H], F32, name="w1_raw", tag="w_raw")
+        w1_rows = w1.rearrange("(p j) c -> p j c", j=PACK)
+        nc.sync.dma_start(w1_raw[:, 0:1, :], w1_rows[:, 0:1, :])
+        for e in range(2):
+            nc.sync.dma_start(scale_table[e:P:GROUP, :].bitcast(I32), x_scales[0, e:16:2, :].bitcast(I32))
+        nc.sync.dma_start(w1_raw[:, 1:PACK, :], w1_rows[:, 1:PACK, :])
+        word_table = keep.tile([P, T], I32, name="word_table")
+        nc.sync.dma_start(word_table[:], x_words[0].rearrange("p n t -> p (n t)").bitcast(I32))
+        n1_sb = load_list(n1, "n1_sb")
+        n2_sb = load_list(n2, "n2_sb")
+        n3_sb = load_list(n3, "n3_sb")
+        n4_sb = load_list(n4, "n4_sb")
+
+        picked_scales = keep.tile([P, S], U8, name="picked_scales")
+        for a in range(2):
+            nc.vector.tensor_copy(picked_scales[:, halves[a]], scale_table[:].indirect(offs_sb[:, list_halves[a]]))
+        x_plane = keep.tile([P, S], U8, name="x_plane", align_bytes=64)
+        nc.vector.tensor_copy(x_plane[:].bitcast(I32), picked_scales[:].bitcast(I32))
+        for e in range(2):
+            nc.scalar.dma_start(x_plane[2 + e : P : 32, :].bitcast(I32), picked_scales[GROUP + e : P : 32, :].bitcast(I32))
+
+        w1_bf = keep.tile([P, PACK * H], BF16, name="w1_bf", align_bytes=64)
+        deal(nc.vector.tensor_copy, w1_bf, w1_raw)
+        w1_codes = keep.tile([P, H], U32, name="w1_codes", align_bytes=64)
+        w1_plane = keep.tile([P, H], U8, name="w1_plane", align_bytes=64)
+        nc.vector.quantize_mx(out=w1_codes[:].bitcast(FP8X4), scales=w1_plane[:], in_=w1_bf[:])
+
+        w2_raw = keep.tile([P, PACK, N], F32, name="w2_raw", tag="w_raw")
+        nc.sync.dma_start(w2_raw[:], w2.rearrange("(p j) c -> p j c", j=PACK))
+
+        gain = keep.tile([P, PACK], F32, name="gain", tag="w1_bf", align_bytes=64)
+        nc.sync.dma_start(gain[:], gn.rearrange("(p t) o -> p (t o)", t=PACK))
+
+        x_codes = keep.tile([P, S], U32, name="x_codes", align_bytes=64)
+        for a in range(2):
+            nc.vector.tensor_copy(x_codes[:, halves[a]], word_table[:].bitcast(U32).indirect(offs_sb[:, list_halves[a]]))
+
+        y = [keep.tile([P, S], F32, name="y%d" % t) for t in range(PACK)]
+        y_order = [(0, 0), (1, 0), (0, 1), (1, 1), (2, 0), (2, 1), (3, 0), (3, 1)]
+        for t, a in y_order:
+            acc = psum.tile([P, HALF], F32, name="y_acc", tag="bank%d" % (2 * t + a))
+            rows = slice(t * P, (t + 1) * P)
+            nc.tensor.matmul_mx(
+                out=acc[:],
+                lhsT=w1_codes[:, rows].bitcast(FP8X4),
+                lhsT_scale=w1_plane[:, rows],
+                rhs=x_codes[:, halves[a]].bitcast(FP8X4),
+                rhs_scale=x_plane[:, halves[a]],
+                start=True,
+                stop=True,
+            )
+            nc.scalar.copy(y[t][:, halves[a]], acc[:])
+
+        w2_bf = keep.tile([P, PACK * N], BF16, name="w2_bf", align_bytes=64)
+        deal(nc.scalar.copy, w2_bf, w2_raw)
+
+        z_bf = [keep.tile([P, HALF, PACK], BF16, name="z_bf%d" % a, align_bytes=64) for a in range(2)]
+        dt = [keep.tile([P, S], F32, name="dt%d" % t, align_bytes=64) for t in range(PACK)]
+        w2_codes_first = keep.tile([P, P], U32, name="w2_codes_first", align_bytes=64)
+        w2_plane_first = keep.tile([P, P], U8, name="w2_plane_first", align_bytes=64)
+        for pair in range(2):
+            tiles = (2 * pair, 2 * pair + 1)
+            pa, pb = {}, {}
+            for t in tiles:
+                pa[t] = keep.tile([P, W], F32, name="pa%d" % t)
+                pb[t] = keep.tile([P, W], F32, name="pb%d" % t)
+                nc.vector.tensor_copy(pa[t][:], y[t][:].indirect(n1_sb[:]))
+                nc.vector.tensor_copy(pb[t][:], y[t][:].indirect(n2_sb[:]))
+            if pair == 1:
+                nc.vector.quantize_mx(out=w2_codes_first[:].bitcast(FP8X4), scales=w2_plane_first[:], in_=w2_bf[:, 0 : PACK * P])
+            for t in tiles:
+                nc.vector.tensor_tensor(dt[t][:].indirect(n1_sb[:]), pa[t][:], pb[t][:], ALU.add)
+            for t in tiles:
+                nc.vector.tensor_tensor(dt[t][:].indirect(n2_sb[:]), pa[t][:], pb[t][:], ALU.mult)
+            for t in tiles:
+                for a in range(2):
+                    if pair == 1 and a == 1:
+                        nc.vector.tensor_scalar(z_bf[a][:, :, t], dt[t][:, halves[a]], gain[:, t : t + 1], None, ALU.mult)
+                    else:
+                        nc.scalar.activation(z_bf[a][:, :, t], dt[t][:, halves[a]], COPY, scale=gain[:, t : t + 1])
+
+        z_codes = keep.tile([P, S], U32, name="z_codes", align_bytes=64)
+        z_plane = keep.tile([P, S], U8, name="z_plane", align_bytes=64)
+        for a in range(2):
+            nc.vector.quantize_mx(
+                out=z_codes[:, halves[a]].bitcast(FP8X4),
+                scales=z_plane[:, halves[a]],
+                in_=z_bf[a][:].rearrange("p c t -> p (c t)"),
+            )
+        w2_codes_rest = keep.tile([P, N - P], U32, name="w2_codes_rest", tag="dt3", align_bytes=64)
+        w2_plane_rest = keep.tile([P, N - P], U8, name="w2_plane_rest", align_bytes=64)
+        nc.vector.quantize_mx(out=w2_codes_rest[:, 0:P].bitcast(FP8X4), scales=w2_plane_rest[:, 0:P], in_=w2_bf[:, PACK * P : 2 * PACK * P])
+        nc.vector.quantize_mx(out=w2_codes_rest[:, P:].bitcast(FP8X4), scales=w2_plane_rest[:, P:], in_=w2_bf[:, 2 * PACK * P :])
+
+        out_rows = out.rearrange("(p t) j -> p t j", t=PACK)
+        for t in range(PACK):
+            h = keep.tile([P, S], F32, name="h%d" % t)
+            h_again = keep.tile([P, S], F32, name="h_again%d" % t)
+            if t == 0:
+                lhs, lhs_plane = w2_codes_first[:], w2_plane_first[:]
+                pieces = halves
+            else:
+                lhs, lhs_plane = w2_codes_rest[:, (t - 1) * P : t * P], w2_plane_rest[:, (t - 1) * P : t * P]
+                pieces = [slice(0, S)]
+            for a, cols in enumerate(pieces):
+                acc = psum.tile([P, cols.stop - cols.start], F32, name="h_acc", tag="bank%d" % (2 * t + a))
+                nc.tensor.matmul_mx(
+                    out=acc[:],
+                    lhsT=lhs.bitcast(FP8X4),
+                    lhsT_scale=lhs_plane,
+                    rhs=z_codes[:, cols].bitcast(FP8X4),
+                    rhs_scale=z_plane[:, cols],
+                    start=True,
+                    stop=True,
+                )
+                nc.scalar.copy(h[:, cols], acc[:])
+                nc.scalar.copy(h_again[:, cols], acc[:])
+            d3 = keep.tile([P, S], F32, name="d3_%d" % t)
+            d4 = keep.tile([P, S], F32, name="d4_%d" % t)
+            res = keep.tile([P, S], F32, name="res%d" % t)
+            for a in range(2):
+                nc.vector.tensor_tensor(d3[:, halves[a]], h[:].indirect(n3_sb[:, list_halves[a]]), h_again[:, halves[a]], ALU.subtract)
+                nc.vector.tensor_tensor(d4[:, halves[a]], h[:].indirect(n4_sb[:, list_halves[a]]), h_again[:, halves[a]], ALU.subtract)
+            for a in range(2):
+                nc.vector.scalar_tensor_tensor(res[:, halves[a]], d3[:, halves[a]], 0.75, d4[:, halves[a]], ALU.mult, ALU.mult)
+                nc.sync.dma_start(out_rows[:, t, halves[a]], res[:, halves[a]])

@@ -19,6 +19,7 @@ P = 128
 PACK = 4
 HALF = S // 2
 GROUP = 16
+LEAD = 512
 
 
 def tile_picked_hashbondquad_none_p_kernel(tc, x_words, x_scales, w1, gn, w2, offs, n1, n2, n3, n4, out):
@@ -35,23 +36,24 @@ def tile_picked_hashbondquad_none_p_kernel(tc, x_words, x_scales, w1, gn, w2, of
             nc.sync.dma_start(tile[:], src)
             return tile
 
-        def deal(engine_copy, grouped, raw):
+        def deal(engine_copy, grouped, raw, tiles):
             engine_copy(
-                out=grouped[:].rearrange("p (t m j) -> p m t j", t=PACK, j=PACK),
-                in_=raw[:].rearrange("p j (m t) -> p m t j", t=PACK),
+                out=grouped[:].rearrange("p (t m j) -> p m t j", m=P, j=PACK),
+                in_=raw[:].rearrange("p j (m t) -> p m t j", t=PACK)[:, :, tiles, :],
             )
 
-        offs_sb = load_list(offs, "offs_sb")
         scale_table = keep.tile([P, T], U8, name="scale_table")
         nc.vector.memset(scale_table[:].bitcast(I32), 0)
 
         w1_raw = keep.tile([P, PACK, H], F32, name="w1_raw", tag="w_raw")
-        w1_rows = w1.rearrange("(p j) c -> p j c", j=PACK)
-        nc.sync.dma_start(w1_raw[:, 0:1, :], w1_rows[:, 0:1, :])
+        w1_rows = w1.rearrange("(p j) c -> p (j c)", j=PACK)
+        w1_flat = w1_raw[:].rearrange("p j c -> p (j c)")
+        nc.sync.dma_start(w1_flat[:, 0:LEAD], w1_rows[:, 0:LEAD])
+        offs_sb = load_list(offs, "offs_sb")
         for e in range(2):
             nc.sync.dma_start(scale_table[e:P:GROUP, :].bitcast(I32), x_scales[0, e:16:2, :].bitcast(I32))
-        nc.sync.dma_start(w1_raw[:, 1:PACK, :], w1_rows[:, 1:PACK, :])
-        word_table = keep.tile([P, T], I32, name="word_table")
+        nc.sync.dma_start(w1_flat[:, LEAD:], w1_rows[:, LEAD:])
+        word_table = keep.tile([P, T], I32, name="word_table", align_bytes=64)
         nc.sync.dma_start(word_table[:], x_words[0].rearrange("p n t -> p (n t)").bitcast(I32))
         n1_sb = load_list(n1, "n1_sb")
         n2_sb = load_list(n2, "n2_sb")
@@ -59,22 +61,20 @@ def tile_picked_hashbondquad_none_p_kernel(tc, x_words, x_scales, w1, gn, w2, of
         n4_sb = load_list(n4, "n4_sb")
 
         picked_scales = keep.tile([P, S], U8, name="picked_scales")
-        for a in range(2):
-            nc.vector.tensor_copy(picked_scales[:, halves[a]], scale_table[:].indirect(offs_sb[:, list_halves[a]]))
+        nc.vector.tensor_copy(picked_scales[:], scale_table[:].indirect(offs_sb[:]))
         x_plane = keep.tile([P, S], U8, name="x_plane", align_bytes=64)
         nc.vector.tensor_copy(x_plane[:].bitcast(I32), picked_scales[:].bitcast(I32))
         for e in range(2):
             nc.scalar.dma_start(x_plane[2 + e : P : 32, :].bitcast(I32), picked_scales[GROUP + e : P : 32, :].bitcast(I32))
 
         w1_bf = keep.tile([P, PACK * H], BF16, name="w1_bf", align_bytes=64)
-        deal(nc.vector.tensor_copy, w1_bf, w1_raw)
+        deal(nc.vector.tensor_copy, w1_bf, w1_raw, slice(0, PACK))
         w1_codes = keep.tile([P, H], U32, name="w1_codes", align_bytes=64)
         w1_plane = keep.tile([P, H], U8, name="w1_plane", align_bytes=64)
         nc.vector.quantize_mx(out=w1_codes[:].bitcast(FP8X4), scales=w1_plane[:], in_=w1_bf[:])
 
         w2_raw = keep.tile([P, PACK, N], F32, name="w2_raw", tag="w_raw")
         nc.sync.dma_start(w2_raw[:], w2.rearrange("(p j) c -> p j c", j=PACK))
-
         gain = keep.tile([P, PACK], F32, name="gain", tag="w1_bf", align_bytes=64)
         nc.sync.dma_start(gain[:], gn.rearrange("(p t) o -> p (t o)", t=PACK))
 
@@ -82,56 +82,74 @@ def tile_picked_hashbondquad_none_p_kernel(tc, x_words, x_scales, w1, gn, w2, of
         for a in range(2):
             nc.vector.tensor_copy(x_codes[:, halves[a]], word_table[:].bitcast(U32).indirect(offs_sb[:, list_halves[a]]))
 
-        y = [keep.tile([P, S], F32, name="y%d" % t) for t in range(PACK)]
-        y_order = [(0, 0), (1, 0), (0, 1), (1, 1), (2, 0), (2, 1), (3, 0), (3, 1)]
-        for t, a in y_order:
-            acc = psum.tile([P, HALF], F32, name="y_acc", tag="bank%d" % (2 * t + a))
-            rows = slice(t * P, (t + 1) * P)
+        bank_names = ["bank%d" % b for b in range(8)]
+
+        def product_piece(lhs, lhs_plane, rhs, rhs_plane, cols, bank):
+            acc = psum.tile([P, cols.stop - cols.start], F32, name="acc", tag=bank_names[bank])
             nc.tensor.matmul_mx(
                 out=acc[:],
-                lhsT=w1_codes[:, rows].bitcast(FP8X4),
-                lhsT_scale=w1_plane[:, rows],
-                rhs=x_codes[:, halves[a]].bitcast(FP8X4),
-                rhs_scale=x_plane[:, halves[a]],
+                lhsT=lhs.bitcast(FP8X4),
+                lhsT_scale=lhs_plane,
+                rhs=rhs[:, cols].bitcast(FP8X4),
+                rhs_scale=rhs_plane[:, cols],
                 start=True,
                 stop=True,
             )
-            nc.scalar.copy(y[t][:, halves[a]], acc[:])
+            return acc
+
+        y = [keep.tile([P, S], F32, name="y%d" % t) for t in range(PACK)]
+        quarters = [slice(q * P, (q + 1) * P) for q in range(4)]
+        y_pieces = [
+            (0, halves[0], nc.scalar.copy),
+            (1, halves[0], nc.vector.tensor_copy),
+            (0, quarters[2], nc.scalar.copy),
+            (0, quarters[3], nc.scalar.copy),
+            (1, halves[1], nc.scalar.copy),
+            (2, slice(0, S), nc.scalar.copy),
+            (3, slice(0, S), nc.scalar.copy),
+        ]
+        bank = 0
+        for t, cols, copy_out in y_pieces:
+            rows = slice(t * P, (t + 1) * P)
+            acc = product_piece(w1_codes[:, rows], w1_plane[:, rows], x_codes, x_plane, cols, bank)
+            copy_out(y[t][:, cols], acc[:])
+            bank = bank + 1
 
         w2_bf = keep.tile([P, PACK * N], BF16, name="w2_bf", align_bytes=64)
-        deal(nc.scalar.copy, w2_bf, w2_raw)
+        deal(nc.scalar.copy, w2_bf, w2_raw, slice(0, PACK))
 
-        z_bf = [keep.tile([P, HALF, PACK], BF16, name="z_bf%d" % a, align_bytes=64) for a in range(2)]
+        z_pieces = [halves[1], slice(0, P), slice(P, HALF)]
+        z_bf = [keep.tile([P, c.stop - c.start, PACK], BF16, name="z_bf%d" % a, align_bytes=64) for a, c in enumerate(z_pieces)]
         dt = [keep.tile([P, S], F32, name="dt%d" % t, align_bytes=64) for t in range(PACK)]
-        w2_codes_first = keep.tile([P, P], U32, name="w2_codes_first", align_bytes=64)
-        w2_plane_first = keep.tile([P, P], U8, name="w2_plane_first", align_bytes=64)
+        wide = [keep.tile([P, 2 * S], F32, name="wide%d" % t) for t in range(PACK)]
         for pair in range(2):
             tiles = (2 * pair, 2 * pair + 1)
             pa, pb = {}, {}
             for t in tiles:
-                pa[t] = keep.tile([P, W], F32, name="pa%d" % t)
-                pb[t] = keep.tile([P, W], F32, name="pb%d" % t)
-                nc.vector.tensor_copy(pa[t][:], y[t][:].indirect(n1_sb[:]))
-                nc.vector.tensor_copy(pb[t][:], y[t][:].indirect(n2_sb[:]))
-            if pair == 1:
-                nc.vector.quantize_mx(out=w2_codes_first[:].bitcast(FP8X4), scales=w2_plane_first[:], in_=w2_bf[:, 0 : PACK * P])
+                pa[t] = wide[t][:, S : S + W]
+                pb[t] = wide[t][:, S + W :]
+                nc.vector.tensor_copy(pa[t], y[t][:].indirect(n1_sb[:]))
+                nc.vector.tensor_copy(pb[t], y[t][:].indirect(n2_sb[:]))
             for t in tiles:
-                nc.vector.tensor_tensor(dt[t][:].indirect(n1_sb[:]), pa[t][:], pb[t][:], ALU.add)
+                nc.vector.tensor_tensor(dt[t][:].indirect(n1_sb[:]), pa[t], pb[t], ALU.add)
             for t in tiles:
-                nc.vector.tensor_tensor(dt[t][:].indirect(n2_sb[:]), pa[t][:], pb[t][:], ALU.mult)
+                nc.vector.tensor_tensor(dt[t][:].indirect(n2_sb[:]), pa[t], pb[t], ALU.mult)
             for t in tiles:
-                for a in range(2):
-                    if pair == 1 and a == 1:
-                        nc.vector.tensor_scalar(z_bf[a][:, :, t], dt[t][:, halves[a]], gain[:, t : t + 1], None, ALU.mult)
+                for a, cols in enumerate(z_pieces):
+                    if pair == 1 and a == 0:
+                        nc.vector.tensor_scalar(z_bf[a][:, :, t], dt[t][:, cols], gain[:, t : t + 1], None, ALU.mult)
                     else:
-                        nc.scalar.activation(z_bf[a][:, :, t], dt[t][:, halves[a]], COPY, scale=gain[:, t : t + 1])
+                        nc.scalar.activation(z_bf[a][:, :, t], dt[t][:, cols], COPY, scale=gain[:, t : t + 1])
 
+        w2_codes_first = keep.tile([P, P], U32, name="w2_codes_first", tag="dt2", align_bytes=64)
+        w2_plane_first = keep.tile([P, P], U8, name="w2_plane_first", align_bytes=64)
+        nc.vector.quantize_mx(out=w2_codes_first[:].bitcast(FP8X4), scales=w2_plane_first[:], in_=w2_bf[:, 0 : PACK * P])
         z_codes = keep.tile([P, S], U32, name="z_codes", align_bytes=64)
         z_plane = keep.tile([P, S], U8, name="z_plane", align_bytes=64)
-        for a in range(2):
+        for a, cols in enumerate(z_pieces):
             nc.vector.quantize_mx(
-                out=z_codes[:, halves[a]].bitcast(FP8X4),
-                scales=z_plane[:, halves[a]],
+                out=z_codes[:, cols].bitcast(FP8X4),
+                scales=z_plane[:, cols],
                 in_=z_bf[a][:].rearrange("p c t -> p (c t)"),
             )
         w2_codes_rest = keep.tile([P, N - P], U32, name="w2_codes_rest", tag="dt3", align_bytes=64)
@@ -140,34 +158,39 @@ def tile_picked_hashbondquad_none_p_kernel(tc, x_words, x_scales, w1, gn, w2, of
         nc.vector.quantize_mx(out=w2_codes_rest[:, P:].bitcast(FP8X4), scales=w2_plane_rest[:, P:], in_=w2_bf[:, 2 * PACK * P :])
 
         out_rows = out.rearrange("(p t) j -> p t j", t=PACK)
-        for t in range(PACK):
-            h = keep.tile([P, S], F32, name="h%d" % t)
-            h_again = keep.tile([P, S], F32, name="h_again%d" % t)
-            if t == 0:
-                lhs, lhs_plane = w2_codes_first[:], w2_plane_first[:]
-                pieces = halves
-            else:
-                lhs, lhs_plane = w2_codes_rest[:, (t - 1) * P : t * P], w2_plane_rest[:, (t - 1) * P : t * P]
-                pieces = [slice(0, S)]
-            for a, cols in enumerate(pieces):
-                acc = psum.tile([P, cols.stop - cols.start], F32, name="h_acc", tag="bank%d" % (2 * t + a))
-                nc.tensor.matmul_mx(
-                    out=acc[:],
-                    lhsT=lhs.bitcast(FP8X4),
-                    lhsT_scale=lhs_plane,
-                    rhs=z_codes[:, cols].bitcast(FP8X4),
-                    rhs_scale=z_plane[:, cols],
-                    start=True,
-                    stop=True,
-                )
-                nc.scalar.copy(h[:, cols], acc[:])
-                nc.scalar.copy(h_again[:, cols], acc[:])
-            d3 = keep.tile([P, S], F32, name="d3_%d" % t)
-            d4 = keep.tile([P, S], F32, name="d4_%d" % t)
-            res = keep.tile([P, S], F32, name="res%d" % t)
-            for a in range(2):
-                nc.vector.tensor_tensor(d3[:, halves[a]], h[:].indirect(n3_sb[:, list_halves[a]]), h_again[:, halves[a]], ALU.subtract)
-                nc.vector.tensor_tensor(d4[:, halves[a]], h[:].indirect(n4_sb[:, list_halves[a]]), h_again[:, halves[a]], ALU.subtract)
-            for a in range(2):
-                nc.vector.scalar_tensor_tensor(res[:, halves[a]], d3[:, halves[a]], 0.75, d4[:, halves[a]], ALU.mult, ALU.mult)
-                nc.sync.dma_start(out_rows[:, t, halves[a]], res[:, halves[a]])
+        whole = slice(0, S)
+        h_again = [keep.tile([P, S], F32, name="h_again%d" % t) for t in range(PACK)]
+        d3 = [keep.tile([P, S], F32, name="d3_%d" % t) for t in range(PACK)]
+        d4 = [keep.tile([P, S], F32, name="d4_%d" % t) for t in range(PACK)]
+        res = [keep.tile([P, S], F32, name="res%d" % t) for t in range(PACK)]
+        for cols in z_pieces:
+            acc = product_piece(w2_codes_first[:], w2_plane_first[:], z_codes, z_plane, cols, bank % 8)
+            nc.scalar.copy(wide[0][:, cols], acc[:])
+            bank = bank + 1
+        nc.vector.tensor_copy(h_again[0][:, halves[1]], wide[0][:, halves[1]])
+        nc.scalar.copy(h_again[0][:, halves[0]], wide[0][:, halves[0]])
+        for t in range(1, PACK):
+            rows = slice((t - 1) * P, t * P)
+            acc = product_piece(w2_codes_rest[:, rows], w2_plane_rest[:, rows], z_codes, z_plane, whole, bank % 8)
+            nc.scalar.copy(wide[t][:, whole], acc[:])
+            nc.scalar.copy(h_again[t][:], acc[:])
+            bank = bank + 1
+
+        def difference(dst, places, t, cols):
+            entries = slice(cols.start // GROUP, cols.stop // GROUP)
+            nc.vector.tensor_tensor(dst[t][:, cols], wide[t][:].indirect(places[:, entries]), h_again[t][:, cols], ALU.subtract)
+
+        def product(t, cols):
+            nc.vector.scalar_tensor_tensor(res[t][:, cols], d3[t][:, cols], 0.75, d4[t][:, cols], ALU.mult, ALU.mult)
+            nc.sync.dma_start(out_rows[:, t, cols], res[t][:, cols])
+
+        difference(d3, n3_sb, 0, halves[1])
+        difference(d3, n3_sb, 0, halves[0])
+        for t in range(PACK - 1):
+            difference(d4, n4_sb, t, whole)
+            difference(d3, n3_sb, t + 1, whole)
+            product(t, whole)
+        for cols in halves:
+            difference(d4, n4_sb, PACK - 1, cols)
+        for cols in halves:
+            product(PACK - 1, cols)

@@ -19,7 +19,7 @@ P = 128
 PACK = 4
 HALF = S // 2
 GROUP = 16
-LEAD = 512
+LEAD = 1024
 
 
 def tile_picked_hashbondquad_none_p_kernel(tc, x_words, x_scales, w1, gn, w2, offs, n1, n2, n3, n4, out):
@@ -65,22 +65,29 @@ def tile_picked_hashbondquad_none_p_kernel(tc, x_words, x_scales, w1, gn, w2, of
         x_plane = keep.tile([P, S], U8, name="x_plane", align_bytes=64)
         nc.vector.tensor_copy(x_plane[:].bitcast(I32), picked_scales[:].bitcast(I32))
         for e in range(2):
-            nc.scalar.dma_start(x_plane[2 + e : P : 32, :].bitcast(I32), picked_scales[GROUP + e : P : 32, :].bitcast(I32))
+            nc.sync.dma_start(x_plane[2 + e : P : 32, :].bitcast(I32), picked_scales[GROUP + e : P : 32, :].bitcast(I32))
 
-        w1_bf = keep.tile([P, PACK * H], BF16, name="w1_bf", align_bytes=64)
-        deal(nc.vector.tensor_copy, w1_bf, w1_raw, slice(0, PACK))
-        w1_codes = keep.tile([P, H], U32, name="w1_codes", align_bytes=64)
-        w1_plane = keep.tile([P, H], U8, name="w1_plane", align_bytes=64)
-        nc.vector.quantize_mx(out=w1_codes[:].bitcast(FP8X4), scales=w1_plane[:], in_=w1_bf[:])
+        w1_bf = [keep.tile([P, 2 * PACK * P], BF16, name="w1_bf%d" % pair, align_bytes=64) for pair in range(2)]
+        deal(nc.vector.tensor_copy, w1_bf[0], w1_raw, slice(0, 2))
+        deal(nc.scalar.copy, w1_bf[1], w1_raw, slice(2, 4))
+
+        def quantise_w1(pair, tag):
+            codes = keep.tile([P, 2 * P], U32, name="w1_codes%d" % pair, tag=tag, align_bytes=64)
+            plane = keep.tile([P, 2 * P], U8, name="w1_plane%d" % pair, align_bytes=64)
+            nc.vector.quantize_mx(out=codes[:].bitcast(FP8X4), scales=plane[:], in_=w1_bf[pair][:])
+            return codes, plane
+
+        w1_mx = [quantise_w1(0, "w1_codes0")]
 
         w2_raw = keep.tile([P, PACK, N], F32, name="w2_raw", tag="w_raw")
         nc.sync.dma_start(w2_raw[:], w2.rearrange("(p j) c -> p j c", j=PACK))
-        gain = keep.tile([P, PACK], F32, name="gain", tag="w1_bf", align_bytes=64)
+        gain = keep.tile([P, PACK], F32, name="gain", tag="w1_bf0", align_bytes=64)
         nc.sync.dma_start(gain[:], gn.rearrange("(p t) o -> p (t o)", t=PACK))
 
         x_codes = keep.tile([P, S], U32, name="x_codes", align_bytes=64)
         for a in range(2):
             nc.vector.tensor_copy(x_codes[:, halves[a]], word_table[:].bitcast(U32).indirect(offs_sb[:, list_halves[a]]))
+        w1_mx.append(quantise_w1(1, "word_table"))
 
         bank_names = ["bank%d" % b for b in range(8)]
 
@@ -110,8 +117,9 @@ def tile_picked_hashbondquad_none_p_kernel(tc, x_words, x_scales, w1, gn, w2, of
         ]
         bank = 0
         for t, cols, copy_out in y_pieces:
-            rows = slice(t * P, (t + 1) * P)
-            acc = product_piece(w1_codes[:, rows], w1_plane[:, rows], x_codes, x_plane, cols, bank)
+            codes, plane = w1_mx[t // 2]
+            rows = slice(t % 2 * P, (t % 2 + 1) * P)
+            acc = product_piece(codes[:, rows], plane[:, rows], x_codes, x_plane, cols, bank)
             copy_out(y[t][:, cols], acc[:])
             bank = bank + 1
 

from contextlib import ExitStack

import concourse.mybir as mybir

K, T, S, N, H, W = 512, 2048, 512, 512, 512, 256
FLOPS = 2 * K * H * S + 2 * H * N * S

F32 = mybir.dt.float32
BF16 = mybir.dt.bfloat16
I32 = mybir.dt.int32
U32 = mybir.dt.uint32
U16 = mybir.dt.uint16
U8 = mybir.dt.uint8
FP8X4 = mybir.dt.float8_e4m3fn_x4
ALU = mybir.AluOpType
COPY = mybir.ActivationFunctionType.Copy

P = 128
PACK = 4
HALF = S // 2
GROUP = 16
LEAD = 1024


def tile_picked_hashbondquad_none_p_kernel(tc, x_words, x_scales, w1, gn, w2, offs, n1, n2, n3, n4, out):
    nc = tc.nc
    halves = [slice(0, HALF), slice(HALF, S)]
    list_halves = [slice(0, HALF // GROUP), slice(HALF // GROUP, S // GROUP)]

    with ExitStack() as ctx:
        keep = ctx.enter_context(tc.tile_pool(name="keep", bufs=1))
        psum = ctx.enter_context(tc.psum_pool(name="psum", bufs=1))

        def load_list(src, name):
            tile = keep.tile(list(src.shape), U16, name=name)
            nc.sync.dma_start(tile[:], src)
            return tile

        def deal(engine_copy, grouped, raw, tiles):
            engine_copy(
                out=grouped[:].rearrange("p (t m j) -> p m t j", m=P, j=PACK),
                in_=raw[:].rearrange("p j (m t) -> p m t j", t=PACK)[:, :, tiles, :],
            )

        scale_table = keep.tile([P, T], U8, name="scale_table")
        nc.vector.memset(scale_table[:].bitcast(I32), 0)

        w1_raw = keep.tile([P, PACK, H], F32, name="w1_raw", tag="w_raw")
        w1_rows = w1.rearrange("(p j) c -> p (j c)", j=PACK)
        w1_flat = w1_raw[:].rearrange("p j c -> p (j c)")
        nc.sync.dma_start(w1_flat[:, 0:LEAD], w1_rows[:, 0:LEAD])
        offs_sb = load_list(offs, "offs_sb")
        for e in range(2):
            nc.sync.dma_start(scale_table[e:P:GROUP, :].bitcast(I32), x_scales[0, e:16:2, :].bitcast(I32))
        nc.sync.dma_start(w1_flat[:, LEAD:], w1_rows[:, LEAD:])
        word_table = keep.tile([P, T], I32, name="word_table", align_bytes=64)
        nc.sync.dma_start(word_table[:], x_words[0].rearrange("p n t -> p (n t)").bitcast(I32))
        n1_sb = load_list(n1, "n1_sb")
        n2_sb = load_list(n2, "n2_sb")
        n3_sb = load_list(n3, "n3_sb")
        n4_sb = load_list(n4, "n4_sb")

        picked_scales = keep.tile([P, S], U8, name="picked_scales")
        nc.vector.tensor_copy(picked_scales[:], scale_table[:].indirect(offs_sb[:]))
        x_plane = keep.tile([P, S], U8, name="x_plane", align_bytes=64)
        nc.vector.tensor_copy(x_plane[:].bitcast(I32), picked_scales[:].bitcast(I32))
        for e in range(2):
            nc.sync.dma_start(x_plane[2 + e : P : 32, :].bitcast(I32), picked_scales[GROUP + e : P : 32, :].bitcast(I32))

        w1_bf = [keep.tile([P, 2 * PACK * P], BF16, name="w1_bf%d" % pair, align_bytes=64) for pair in range(2)]
        deal(nc.vector.tensor_copy, w1_bf[0], w1_raw, slice(0, 2))
        deal(nc.scalar.copy, w1_bf[1], w1_raw, slice(2, 4))

        def quantise_w1(pair, tag):
            codes = keep.tile([P, 2 * P], U32, name="w1_codes%d" % pair, tag=tag, align_bytes=64)
            plane = keep.tile([P, 2 * P], U8, name="w1_plane%d" % pair, align_bytes=64)
            nc.vector.quantize_mx(out=codes[:].bitcast(FP8X4), scales=plane[:], in_=w1_bf[pair][:])
            return codes, plane

        w1_mx = [quantise_w1(0, "w1_codes0")]

        w2_raw = keep.tile([P, PACK, N], F32, name="w2_raw", tag="w_raw")
        nc.sync.dma_start(w2_raw[:], w2.rearrange("(p j) c -> p j c", j=PACK))
        gain = keep.tile([P, PACK], F32, name="gain", tag="w1_bf0", align_bytes=64)
        nc.sync.dma_start(gain[:], gn.rearrange("(p t) o -> p (t o)", t=PACK))

        x_codes = keep.tile([P, S], U32, name="x_codes", align_bytes=64)
        for a in range(2):
            nc.vector.tensor_copy(x_codes[:, halves[a]], word_table[:].bitcast(U32).indirect(offs_sb[:, list_halves[a]]))
        w1_mx.append(quantise_w1(1, "word_table"))

        bank_names = ["bank%d" % b for b in range(8)]

        def product_piece(lhs, lhs_plane, rhs, rhs_plane, cols, bank):
            acc = psum.tile([P, cols.stop - cols.start], F32, name="acc", tag=bank_names[bank])
            nc.tensor.matmul_mx(
                out=acc[:],
                lhsT=lhs.bitcast(FP8X4),
                lhsT_scale=lhs_plane,
                rhs=rhs[:, cols].bitcast(FP8X4),
                rhs_scale=rhs_plane[:, cols],
                start=True,
                stop=True,
            )
            return acc

        y = [keep.tile([P, S], F32, name="y%d" % t) for t in range(PACK)]
        quarters = [slice(q * P, (q + 1) * P) for q in range(4)]
        y_pieces = [
            (0, halves[0], nc.scalar.copy),
            (1, halves[0], nc.vector.tensor_copy),
            (0, quarters[2], nc.scalar.copy),
            (0, quarters[3], nc.scalar.copy),
            (1, halves[1], nc.scalar.copy),
            (2, slice(0, S), nc.scalar.copy),
            (3, slice(0, S), nc.scalar.copy),
        ]
        bank = 0
        for t, cols, copy_out in y_pieces:
            codes, plane = w1_mx[t // 2]
            rows = slice(t % 2 * P, (t % 2 + 1) * P)
            acc = product_piece(codes[:, rows], plane[:, rows], x_codes, x_plane, cols, bank)
            copy_out(y[t][:, cols], acc[:])
            bank = bank + 1

        w2_bf = keep.tile([P, PACK * N], BF16, name="w2_bf", align_bytes=64)
        deal(nc.scalar.copy, w2_bf, w2_raw, slice(0, PACK))

        z_pieces = [halves[1], slice(0, P), slice(P, HALF)]
        z_bf = [keep.tile([P, c.stop - c.start, PACK], BF16, name="z_bf%d" % a, align_bytes=64) for a, c in enumerate(z_pieces)]
        dt = [keep.tile([P, S], F32, name="dt%d" % t, align_bytes=64) for t in range(PACK)]
        wide = [keep.tile([P, 2 * S], F32, name="wide%d" % t) for t in range(PACK)]
        for pair in range(2):
            tiles = (2 * pair, 2 * pair + 1)
            pa, pb = {}, {}
            for t in tiles:
                pa[t] = wide[t][:, S : S + W]
                pb[t] = wide[t][:, S + W :]
                nc.vector.tensor_copy(pa[t], y[t][:].indirect(n1_sb[:]))
                nc.vector.tensor_copy(pb[t], y[t][:].indirect(n2_sb[:]))
            for t in tiles:
                nc.vector.tensor_tensor(dt[t][:].indirect(n1_sb[:]), pa[t], pb[t], ALU.add)
            for t in tiles:
                nc.vector.tensor_tensor(dt[t][:].indirect(n2_sb[:]), pa[t], pb[t], ALU.mult)
            for t in tiles:
                for a, cols in enumerate(z_pieces):
                    if pair == 1 and a == 0:
                        nc.vector.tensor_scalar(z_bf[a][:, :, t], dt[t][:, cols], gain[:, t : t + 1], None, ALU.mult)
                    else:
                        nc.scalar.activation(z_bf[a][:, :, t], dt[t][:, cols], COPY, scale=gain[:, t : t + 1])

        w2_codes_first = keep.tile([P, P], U32, name="w2_codes_first", tag="dt2", align_bytes=64)
        w2_plane_first = keep.tile([P, P], U8, name="w2_plane_first", align_bytes=64)
        nc.vector.quantize_mx(out=w2_codes_first[:].bitcast(FP8X4), scales=w2_plane_first[:], in_=w2_bf[:, 0 : PACK * P])
        z_codes = keep.tile([P, S], U32, name="z_codes", align_bytes=64)
        z_plane = keep.tile([P, S], U8, name="z_plane", align_bytes=64)
        for a, cols in enumerate(z_pieces):
            nc.vector.quantize_mx(
                out=z_codes[:, cols].bitcast(FP8X4),
                scales=z_plane[:, cols],
                in_=z_bf[a][:].rearrange("p c t -> p (c t)"),
            )
        w2_codes_rest = keep.tile([P, N - P], U32, name="w2_codes_rest", tag="dt3", align_bytes=64)
        w2_plane_rest = keep.tile([P, N - P], U8, name="w2_plane_rest", align_bytes=64)
        nc.vector.quantize_mx(out=w2_codes_rest[:, 0:P].bitcast(FP8X4), scales=w2_plane_rest[:, 0:P], in_=w2_bf[:, PACK * P : 2 * PACK * P])
        nc.vector.quantize_mx(out=w2_codes_rest[:, P:].bitcast(FP8X4), scales=w2_plane_rest[:, P:], in_=w2_bf[:, 2 * PACK * P :])

        out_rows = out.rearrange("(p t) j -> p t j", t=PACK)
        whole = slice(0, S)
        h_again = [keep.tile([P, S], F32, name="h_again%d" % t) for t in range(PACK)]
        d3 = [keep.tile([P, S], F32, name="d3_%d" % t) for t in range(PACK)]
        d4 = [keep.tile([P, S], F32, name="d4_%d" % t) for t in range(PACK)]
        res = [keep.tile([P, S], F32, name="res%d" % t) for t in range(PACK)]
        for cols in z_pieces:
            acc = product_piece(w2_codes_first[:], w2_plane_first[:], z_codes, z_plane, cols, bank % 8)
            nc.scalar.copy(wide[0][:, cols], acc[:])
            bank = bank + 1
        nc.vector.tensor_copy(h_again[0][:, halves[1]], wide[0][:, halves[1]])
        nc.scalar.copy(h_again[0][:, halves[0]], wide[0][:, halves[0]])
        for t in range(1, PACK):
            rows = slice((t - 1) * P, t * P)
            acc = product_piece(w2_codes_rest[:, rows], w2_plane_rest[:, rows], z_codes, z_plane, whole, bank % 8)
            nc.scalar.copy(wide[t][:, whole], acc[:])
            nc.scalar.copy(h_again[t][:], acc[:])
            bank = bank + 1

        def difference(dst, places, t, cols):
            entries = slice(cols.start // GROUP, cols.stop // GROUP)
            nc.vector.tensor_tensor(dst[t][:, cols], wide[t][:].indirect(places[:, entries]), h_again[t][:, cols], ALU.subtract)

        def product(t, cols):
            nc.vector.scalar_tensor_tensor(res[t][:, cols], d3[t][:, cols], 0.75, d4[t][:, cols], ALU.mult, ALU.mult)
            nc.sync.dma_start(out_rows[:, t, cols], res[t][:, cols])

        difference(d3, n3_sb, 0, halves[1])
        difference(d3, n3_sb, 0, halves[0])
        for t in range(PACK - 1):
            difference(d4, n4_sb, t, whole)
            difference(d3, n3_sb, t + 1, whole)
            product(t, whole)
        for cols in halves:
            difference(d4, n4_sb, PACK - 1, cols)
        for cols in halves:
            product(PACK - 1, cols)
